import numpy as np
import ml_dtypes


def mxq(x, axis, fmt="e4m3"):
    dtype, down = {"e4m3": (ml_dtypes.float8_e4m3fn, 7), "e5m2": (ml_dtypes.float8_e5m2, 14)}[fmt]
    v = np.moveaxis(np.asarray(x, np.float32).astype(ml_dtypes.bfloat16).astype(np.float64), axis, -1)
    blocks = v.reshape(v.shape[:-1] + (-1, 32))
    amax = np.abs(blocks).max(-1, keepdims=True)
    byte = np.maximum(np.where(amax > 0, np.frexp(amax)[1] - 1 + 127, 0) - down, 1)
    scale = np.exp2(byte - 127.0)
    codes = (blocks / scale).astype(np.float32).astype(dtype).astype(np.float64)
    return np.moveaxis((codes * scale).reshape(v.shape), -1, axis)


WIDE = False


def mx_kscale(k):
    if not WIDE:
        return np.ones(k)
    levels = np.array([10, -10, 5, -5, 0])
    if k % 512:
        return np.exp2(np.random.permutation(np.resize(levels, k // 32))).repeat(32)
    a = np.empty((k // 512, 16))
    for p in range(k // 512):
        a[p, :8] = np.random.permutation(np.resize(levels, 8))
        for g in range(8):
            far = levels[np.abs(levels - a[p, g]) >= 10]
            a[p, g + 8] = far[np.random.randint(len(far))]
    return np.exp2(a.ravel()).repeat(32)


def f64(x):
    return np.asarray(x).astype(np.float64)


def striped(idx):
    return np.tile(np.asarray(idx).reshape(-1, 16).T, (8, 1)).astype(np.uint16)


def unstriped(offs):
    return offs[:16].T.reshape(-1).astype(np.int64)


B, N, T, D, DV, NQ = 1, 512, 2048, 512, 0, 256
PAGE = 32
SEG = 32


def setup_inputs():
    n = np.random.standard_normal
    pages = np.random.permutation(T // PAGE)[:B * N // PAGE]
    idx = (pages[:, None] * PAGE + np.arange(PAGE)[None, :]).reshape(-1)
    s = mx_kscale(D)[:, None]
    return {
        "qT": (n((B, D, NQ)) * s * (1.00 / np.sqrt(D))).astype(np.float32),
        "kT": (n((D, T)) / s).astype(np.float32),
        "kb": np.tile(n(T), (128, 1)).astype(np.float32),
        "offs": striped(idx),
    }


def reference(qT, kT, kb, offs):
    idx = unstriped(offs)
    pick = lambda x: x[:, idx].reshape(x.shape[0], B, N).transpose(1, 0, 2)
    a = mxq(f64(qT), 1, "e4m3").transpose(0, 2, 1) @ mxq(pick(f64(kT)), 1, "e4m3")
    a = a + pick(f64(kb))[:, :1, :]
    return a.reshape(B, NQ, N // SEG, SEG).max(-1)

@@ -1,0 +1,103 @@
+from contextlib import ExitStack
+
+import concourse.mybir as mybir
+from concourse.masks import make_identity
+
+D, T, N, NQ, PAGE = 512, 2048, 512, 256, 32
+P = 128
+PACK = 4
+CHUNK = 128
+CHUNKS = N // CHUNK
+
+F32 = mybir.dt.float32
+BF16 = mybir.dt.bfloat16
+U32 = mybir.dt.uint32
+U16 = mybir.dt.uint16
+U8 = mybir.dt.uint8
+FP8X4 = mybir.dt.float8_e4m3fn_x4
+IDENTITY = mybir.ActivationFunctionType.Identity
+
+FLOPS = 2 * NQ * N * D
+BYTES = 4 * (D * NQ + D * T + T + NQ * N // PAGE) + 2 * P * N // 16
+
+
+def tile_attend_maxsim_kb_kernel(tc, qT, kT, kb, offs, out):
+    nc = tc.nc
+    with ExitStack() as ctx:
+        held = ctx.enter_context(tc.tile_pool(name="held", bufs=1))
+        psum = ctx.enter_context(tc.psum_pool(name="psum", bufs=1))
+
+        offsets = held.tile([P, N // 16], U16, name="offsets")
+        nc.sync.dma_start(offsets[:], offs)
+
+        kb_row = held.tile([P, T], F32, name="kb_row")
+        nc.vector.memset(kb_row[:], 0.0)
+
+        kT_planes = kT.rearrange("(p t) n -> p t n", t=PACK)
+        planes = []
+        for t in range(PACK):
+            plane = held.tile([P, T], F32, name="plane%d" % t)
+            planes.append(plane)
+        q_raw = held.tile([P, PACK, NQ], F32, name="q_raw")
+        nc.sync.dma_start(planes[0][:], kT_planes[:, 0, :])
+        nc.sync.dma_start(kb_row[0:1, :], kb[0:1, :])
+        for t in range(1, PACK - 1):
+            nc.sync.dma_start(planes[t][:], kT_planes[:, t, :])
+        nc.sync.dma_start(q_raw[:], qT[0].rearrange("(p t) q -> p t q", t=PACK))
+        nc.sync.dma_start(planes[PACK - 1][:], kT_planes[:, PACK - 1, :])
+
+        identity = held.tile([P, P], F32, name="identity")
+        make_identity(nc, identity[:])
+
+        kb_listed = held.tile([P, N], F32, name="kb_listed")
+        nc.vector.tensor_copy(kb_listed[:], kb_row[:].indirect(offsets[:]))
+        kb_turned = psum.tile([P, CHUNKS, P], F32, name="kb_turned")
+        for s in range(CHUNKS):
+            nc.tensor.transpose(kb_turned[:, s, :], kb_listed[:, s * CHUNK : (s + 1) * CHUNK], identity[:])
+        bias = held.tile([P, CHUNKS], F32, name="bias")
+        nc.scalar.copy(bias[:], kb_turned[:, :, 0])
+
+        keys = held.tile([P, N, PACK], BF16, name="keys", align_bytes=64)
+        for t in range(PACK - 1):
+            nc.vector.tensor_copy(keys[:, :, t], planes[t][:].indirect(offsets[:]))
+
+        queries = held.tile([P, NQ, PACK], BF16, name="queries", align_bytes=64)
+        q_codes = held.tile([P, NQ], U32, name="q_codes", align_bytes=64)
+        q_scales = held.tile([P, NQ], U8, name="q_scales", align_bytes=64)
+        nc.scalar.copy(queries[:], q_raw[:].rearrange("p t q -> p q t"))
+        nc.vector.quantize_mx(out=q_codes[:].bitcast(FP8X4), scales=q_scales[:], in_=queries[:].rearrange("p q t -> p (q t)"))
+
+        best = held.tile([P, NQ // P, N // PAGE], F32, name="best")
+        HALF = N // 2
+        t = PACK - 1
+        for h in range(2):
+            cols = slice(h * HALF, (h + 1) * HALF)
+            codes = held.tile([P, HALF], U32, name="k_codes%d" % h, align_bytes=64)
+            scales = held.tile([P, HALF], U8, name="k_scales%d" % h, align_bytes=64)
+            nc.vector.tensor_copy(keys[:, cols, t], planes[t][:].indirect(offsets[:, h * HALF // 16 : (h + 1) * HALF // 16]))
+            nc.vector.quantize_mx(out=codes[:].bitcast(FP8X4), scales=scales[:], in_=keys[:, cols, :].rearrange("p n t -> p (n t)"))
+            for c in range(2):
+                s = 2 * h + c
+                kc = slice(c * CHUNK, (c + 1) * CHUNK)
+                scores = psum.tile([P, NQ], F32, name="scores%d" % s)
+                nc.tensor.matmul_mx(
+                    out=scores[:],
+                    lhsT=codes[:, kc].bitcast(FP8X4),
+                    lhsT_scale=scales[:, kc],
+                    rhs=q_codes[:].bitcast(FP8X4),
+                    rhs_scale=q_scales[:],
+                    start=True,
+                    stop=True,
+                )
+                biased = held.tile([P, NQ], F32, name="biased%d" % s)
+                nc.scalar.activation(biased[:], scores[:], IDENTITY, bias=bias[:, s : s + 1])
+                turned = psum.tile([P, NQ // P, CHUNK], F32, name="turned%d" % min(s, 2))
+                for r in range(NQ // P):
+                    nc.tensor.transpose(turned[:, r, :], biased[:, r * P : (r + 1) * P], identity[:])
+                per = CHUNK // PAGE
+                nc.vector.reduce_max(
+                    best[:, :, s * per : (s + 1) * per],
+                    turned[:].rearrange("p r (j i) -> p r j i", i=PAGE),
+                    axis=mybir.AxisListType.X,
+                )
+        nc.sync.dma_start(out[0].rearrange("(r p) j -> p r j", p=P), best[:])

@@ -41,63 +41,85 @@ def tile_attend_maxsim_kb_kernel(tc, qT, kT, kb, offs, out):
         q_raw = held.tile([P, PACK, NQ], F32, name="q_raw")
         nc.sync.dma_start(planes[0][:], kT_planes[:, 0, :])
         nc.sync.dma_start(kb_row[0:1, :], kb[0:1, :])
-        for t in range(1, PACK - 1):
-            nc.sync.dma_start(planes[t][:], kT_planes[:, t, :])
+        nc.sync.dma_start(planes[1][:], kT_planes[:, 1, :])
         nc.sync.dma_start(q_raw[:], qT[0].rearrange("(p t) q -> p t q", t=PACK))
-        nc.sync.dma_start(planes[PACK - 1][:], kT_planes[:, PACK - 1, :])
+        for t in range(2, PACK):
+            nc.sync.dma_start(planes[t][:], kT_planes[:, t, :])
 
         identity = held.tile([P, P], F32, name="identity")
         make_identity(nc, identity[:])
 
         kb_listed = held.tile([P, N], F32, name="kb_listed")
         nc.vector.tensor_copy(kb_listed[:], kb_row[:].indirect(offsets[:]))
-        kb_turned = psum.tile([P, CHUNKS, P], F32, name="kb_turned")
+        kb_turned = psum.tile([P, CHUNKS, P], F32, name="turned0")
         for s in range(CHUNKS):
             nc.tensor.transpose(kb_turned[:, s, :], kb_listed[:, s * CHUNK : (s + 1) * CHUNK], identity[:])
         bias = held.tile([P, CHUNKS], F32, name="bias")
         nc.scalar.copy(bias[:], kb_turned[:, :, 0])
 
         keys = held.tile([P, N, PACK], BF16, name="keys", align_bytes=64)
-        for t in range(PACK - 1):
-            nc.vector.tensor_copy(keys[:, :, t], planes[t][:].indirect(offsets[:]))
-
         queries = held.tile([P, NQ, PACK], BF16, name="queries", align_bytes=64)
         q_codes = held.tile([P, NQ], U32, name="q_codes", align_bytes=64)
         q_scales = held.tile([P, NQ], U8, name="q_scales", align_bytes=64)
         nc.scalar.copy(queries[:], q_raw[:].rearrange("p t q -> p q t"))
-        nc.vector.quantize_mx(out=q_codes[:].bitcast(FP8X4), scales=q_scales[:], in_=queries[:].rearrange("p q t -> p (q t)"))
+        for t in range(PACK - 1):
+            nc.vector.tensor_copy(keys[:, :, t], planes[t][:].indirect(offsets[:]))
+            if t == 1:
+                nc.vector.quantize_mx(out=q_codes[:].bitcast(FP8X4), scales=q_scales[:], in_=queries[:].rearrange("p q t -> p (q t)"))
 
+        warm = psum.tile([P, 4, P], F32, name="turned3")
+        for t, count in ((2, 12), (3, 8)):
+            for i in range(count):
+                nc.tensor.transpose(warm[:, i % 4, :], planes[t][:, i * P % T : i * P % T + P], identity[:])
         best = held.tile([P, NQ // P, N // PAGE], F32, name="best")
         HALF = N // 2
         t = PACK - 1
+        codes, scales, scores, biased, turned = [], [], [], [], []
         for h in range(2):
             cols = slice(h * HALF, (h + 1) * HALF)
-            codes = held.tile([P, HALF], U32, name="k_codes%d" % h, align_bytes=64)
-            scales = held.tile([P, HALF], U8, name="k_scales%d" % h, align_bytes=64)
+            code = held.tile([P, HALF], U32, name="k_codes%d" % h, align_bytes=64)
+            scale = held.tile([P, HALF], U8, name="k_scales%d" % h, align_bytes=64)
             nc.vector.tensor_copy(keys[:, cols, t], planes[t][:].indirect(offsets[:, h * HALF // 16 : (h + 1) * HALF // 16]))
-            nc.vector.quantize_mx(out=codes[:].bitcast(FP8X4), scales=scales[:], in_=keys[:, cols, :].rearrange("p n t -> p (n t)"))
             for c in range(2):
-                s = 2 * h + c
                 kc = slice(c * CHUNK, (c + 1) * CHUNK)
-                scores = psum.tile([P, NQ], F32, name="scores%d" % s)
-                nc.tensor.matmul_mx(
-                    out=scores[:],
-                    lhsT=codes[:, kc].bitcast(FP8X4),
-                    lhsT_scale=scales[:, kc],
-                    rhs=q_codes[:].bitcast(FP8X4),
-                    rhs_scale=q_scales[:],
-                    start=True,
-                    stop=True,
-                )
-                biased = held.tile([P, NQ], F32, name="biased%d" % s)
-                nc.scalar.activation(biased[:], scores[:], IDENTITY, bias=bias[:, s : s + 1])
-                turned = psum.tile([P, NQ // P, CHUNK], F32, name="turned%d" % min(s, 2))
-                for r in range(NQ // P):
-                    nc.tensor.transpose(turned[:, r, :], biased[:, r * P : (r + 1) * P], identity[:])
-                per = CHUNK // PAGE
-                nc.vector.reduce_max(
-                    best[:, :, s * per : (s + 1) * per],
-                    turned[:].rearrange("p r (j i) -> p r j i", i=PAGE),
-                    axis=mybir.AxisListType.X,
-                )
+                at = h * HALF + c * CHUNK
+                nc.vector.quantize_mx(out=code[:, kc].bitcast(FP8X4), scales=scale[:, kc], in_=keys[:, at : at + CHUNK, :].rearrange("p n t -> p (n t)"))
+            codes.append(code)
+            scales.append(scale)
+        per = CHUNK // PAGE
+
+        def score_chunk(s):
+            kc = slice(s % 2 * CHUNK, (s % 2 + 1) * CHUNK)
+            score = psum.tile([P, NQ], F32, name="scores%d" % s)
+            nc.tensor.matmul_mx(
+                out=score[:],
+                lhsT=codes[s // 2][:, kc].bitcast(FP8X4),
+                lhsT_scale=scales[s // 2][:, kc],
+                rhs=q_codes[:].bitcast(FP8X4),
+                rhs_scale=q_scales[:],
+                start=True,
+                stop=True,
+            )
+            bia = held.tile([P, NQ], F32, name="biased%d" % s)
+            nc.scalar.activation(bia[:], score[:], IDENTITY, bias=bias[:, s : s + 1])
+            biased.append(bia)
+
+        def best_of_chunk(s):
+            turn = psum.tile([P, NQ // P, CHUNK], F32, name="turned%d" % s)
+            for r in range(NQ // P):
+                nc.tensor.transpose(turn[:, r, :], biased[s][:, r * P : (r + 1) * P], identity[:])
+            nc.vector.reduce_max(
+                best[:, :, s * per : (s + 1) * per],
+                turn[:].rearrange("p r (j i) -> p r j i", i=PAGE),
+                axis=mybir.AxisListType.X,
+            )
+
+        score_chunk(0)
+        score_chunk(1)
+        best_of_chunk(0)
+        score_chunk(2)
+        best_of_chunk(1)
+        score_chunk(3)
+        best_of_chunk(2)
+        best_of_chunk(3)
         nc.sync.dma_start(out[0].rearrange("(r p) j -> p r j", p=P), best[:])

from contextlib import ExitStack

import concourse.mybir as mybir
from concourse.masks import make_identity

D, T, N, NQ, PAGE = 512, 2048, 512, 256, 32
P = 128
PACK = 4
CHUNK = 128
CHUNKS = N // CHUNK

F32 = mybir.dt.float32
BF16 = mybir.dt.bfloat16
U32 = mybir.dt.uint32
U16 = mybir.dt.uint16
U8 = mybir.dt.uint8
FP8X4 = mybir.dt.float8_e4m3fn_x4
IDENTITY = mybir.ActivationFunctionType.Identity

FLOPS = 2 * NQ * N * D
BYTES = 4 * (D * NQ + D * T + T + NQ * N // PAGE) + 2 * P * N // 16


def tile_attend_maxsim_kb_kernel(tc, qT, kT, kb, offs, out):
    nc = tc.nc
    with ExitStack() as ctx:
        held = ctx.enter_context(tc.tile_pool(name="held", bufs=1))
        psum = ctx.enter_context(tc.psum_pool(name="psum", bufs=1))

        offsets = held.tile([P, N // 16], U16, name="offsets")
        nc.sync.dma_start(offsets[:], offs)

        kb_row = held.tile([P, T], F32, name="kb_row")
        nc.vector.memset(kb_row[:], 0.0)

        kT_planes = kT.rearrange("(p t) n -> p t n", t=PACK)
        planes = []
        for t in range(PACK):
            plane = held.tile([P, T], F32, name="plane%d" % t)
            planes.append(plane)
        q_raw = held.tile([P, PACK, NQ], F32, name="q_raw")
        nc.sync.dma_start(planes[0][:], kT_planes[:, 0, :])
        nc.sync.dma_start(kb_row[0:1, :], kb[0:1, :])
        nc.sync.dma_start(planes[1][:], kT_planes[:, 1, :])
        nc.sync.dma_start(q_raw[:], qT[0].rearrange("(p t) q -> p t q", t=PACK))
        for t in range(2, PACK):
            nc.sync.dma_start(planes[t][:], kT_planes[:, t, :])

        identity = held.tile([P, P], F32, name="identity")
        make_identity(nc, identity[:])

        kb_listed = held.tile([P, N], F32, name="kb_listed")
        nc.vector.tensor_copy(kb_listed[:], kb_row[:].indirect(offsets[:]))
        kb_turned = psum.tile([P, CHUNKS, P], F32, name="turned0")
        for s in range(CHUNKS):
            nc.tensor.transpose(kb_turned[:, s, :], kb_listed[:, s * CHUNK : (s + 1) * CHUNK], identity[:])
        bias = held.tile([P, CHUNKS], F32, name="bias")
        nc.scalar.copy(bias[:], kb_turned[:, :, 0])

        keys = held.tile([P, N, PACK], BF16, name="keys", align_bytes=64)
        queries = held.tile([P, NQ, PACK], BF16, name="queries", align_bytes=64)
        q_codes = held.tile([P, NQ], U32, name="q_codes", align_bytes=64)
        q_scales = held.tile([P, NQ], U8, name="q_scales", align_bytes=64)
        nc.scalar.copy(queries[:], q_raw[:].rearrange("p t q -> p q t"))
        for t in range(PACK - 1):
            nc.vector.tensor_copy(keys[:, :, t], planes[t][:].indirect(offsets[:]))
            if t == 1:
                nc.vector.quantize_mx(out=q_codes[:].bitcast(FP8X4), scales=q_scales[:], in_=queries[:].rearrange("p q t -> p (q t)"))

        warm = psum.tile([P, 4, P], F32, name="turned3")
        for t, count in ((2, 12), (3, 8)):
            for i in range(count):
                nc.tensor.transpose(warm[:, i % 4, :], planes[t][:, i * P % T : i * P % T + P], identity[:])
        best = held.tile([P, NQ // P, N // PAGE], F32, name="best")
        HALF = N // 2
        t = PACK - 1
        codes, scales, scores, biased, turned = [], [], [], [], []
        for h in range(2):
            cols = slice(h * HALF, (h + 1) * HALF)
            code = held.tile([P, HALF], U32, name="k_codes%d" % h, align_bytes=64)
            scale = held.tile([P, HALF], U8, name="k_scales%d" % h, align_bytes=64)
            nc.vector.tensor_copy(keys[:, cols, t], planes[t][:].indirect(offsets[:, h * HALF // 16 : (h + 1) * HALF // 16]))
            for c in range(2):
                kc = slice(c * CHUNK, (c + 1) * CHUNK)
                at = h * HALF + c * CHUNK
                nc.vector.quantize_mx(out=code[:, kc].bitcast(FP8X4), scales=scale[:, kc], in_=keys[:, at : at + CHUNK, :].rearrange("p n t -> p (n t)"))
            codes.append(code)
            scales.append(scale)
        per = CHUNK // PAGE

        def score_chunk(s):
            kc = slice(s % 2 * CHUNK, (s % 2 + 1) * CHUNK)
            score = psum.tile([P, NQ], F32, name="scores%d" % s)
            nc.tensor.matmul_mx(
                out=score[:],
                lhsT=codes[s // 2][:, kc].bitcast(FP8X4),
                lhsT_scale=scales[s // 2][:, kc],
                rhs=q_codes[:].bitcast(FP8X4),
                rhs_scale=q_scales[:],
                start=True,
                stop=True,
            )
            bia = held.tile([P, NQ], F32, name="biased%d" % s)
            nc.scalar.activation(bia[:], score[:], IDENTITY, bias=bias[:, s : s + 1])
            biased.append(bia)

        def best_of_chunk(s):
            turn = psum.tile([P, NQ // P, CHUNK], F32, name="turned%d" % s)
            for r in range(NQ // P):
                nc.tensor.transpose(turn[:, r, :], biased[s][:, r * P : (r + 1) * P], identity[:])
            nc.vector.reduce_max(
                best[:, :, s * per : (s + 1) * per],
                turn[:].rearrange("p r (j i) -> p r j i", i=PAGE),
                axis=mybir.AxisListType.X,
            )

        score_chunk(0)
        score_chunk(1)
        best_of_chunk(0)
        score_chunk(2)
        best_of_chunk(1)
        score_chunk(3)
        best_of_chunk(2)
        best_of_chunk(3)
        nc.sync.dma_start(out[0].rearrange("(r p) j -> p r j", p=P), best[:])
